import numpy as np, ml_dtypes
CORES = [1,9,17,25,33,41,49,57,129,257,385]
N = 11
KT, F = 1, 512
def setup_inputs(rng):
    return {"a": rng.standard_normal((N, 128, KT * 128), dtype=np.float32).astype(ml_dtypes.bfloat16), "w": rng.standard_normal((N, 128, KT * F), dtype=np.float32).astype(ml_dtypes.bfloat16)}
def reference(a, w):
    tot = np.zeros((128, F))
    for j in range(N):
        for t in range(KT):
            tot += a[j][:, 128 * t:128 * t + 128].astype(np.float64).T @ w[j][:, F * t:F * t + F].astype(np.float64)
    s = tot.astype(ml_dtypes.bfloat16 if a.dtype != np.float64 else np.float64)
    return {"y": np.broadcast_to(s, (N,) + s.shape)}

@@ -1,0 +1,203 @@
+from concourse.bass import DstId, RemoteDMATransfer
+
+S = 4
+W = 512 // S
+ADD = 1
+
+SCRATCH = {
+    "a_sb": ("sbuf", [128, 128], "bfloat16"),
+    "w_sb": ("sbuf", [128, 512], "bfloat16"),
+    "p_sb": ("sbuf", [128, 512], "bfloat16"),
+    "ps0": ("psum", [128, 512], "float32"),
+    "ps1": ("psum", [128, 512], "float32"),
+    "ps2": ("psum", [128, 512], "float32"),
+    "ps3": ("psum", [128, 512], "float32"),
+    "box": ("dram", [5, 128, W], "bfloat16"),
+}
+SEMAPHORES = ["lda", "ldw", "mm0", "mm1", "mm2", "mm3", "cast", "sent", "raw", "sums",
+              "fin0", "fin1", "fin2", "fin3", "stored"]
+
+_CACHE = {}
+
+
+def _bits(mask):
+    return [1 << i for i in range(mask.bit_length()) if (mask >> i) & 1]
+
+
+def _count(mask):
+    return len(_bits(mask))
+
+
+def _join(bits):
+    m = 0
+    for b in bits:
+        m |= b
+    return m
+
+
+def _same_chip(topo, a, b):
+    return topo.host(a) == topo.host(b) and topo.chip(a) == topo.chip(b)
+
+
+def _plan(T, topo):
+    if "plan" in _CACHE:
+        return _CACHE["plan"]
+    ranks = list(T.cores)
+    hosts = list(range(max(topo.host(c) for c in ranks) + 1))
+    world = range(len(hosts) * topo.CORES_PER_HOST)
+    chips = {}
+    for c in world:
+        chips.setdefault((topo.host(c), topo.chip(c)), []).append(c)
+
+    groups = []
+    for c in ranks:
+        home = [grp for grp in groups if topo.same_plane(c, grp[0])]
+        if home:
+            home[0].append(c)
+        else:
+            groups.append([c])
+    groups.sort(key=lambda grp: -len(grp))
+
+    first = {h: chips[(h, 0)][0] for h in hosts}
+    combos = [[]]
+    for grp in groups:
+        near = [h for h in hosts if topo.rack(h) == topo.rack(topo.host(grp[0]))]
+        combos = [c + [h] for c in combos for h in near]
+    combos = [c for c in combos if all(topo.may_write(first[x], first[y]) for x in c for y in c)]
+    hub = max(combos, key=lambda c: sum(topo.host(r) == h for grp, h in zip(groups, c) for r in grp))
+
+    seats = []
+    for gi, grp in enumerate(groups):
+        cand = [cs for (h, k), cs in sorted(chips.items()) if h == hub[gi]
+                and all(_same_chip(topo, r, cs[0]) or topo.same_plane(r, cs[0]) for r in grp)]
+        if gi == 0:
+            cand.sort(key=lambda cs: not any(r in cs for r in grp))
+            seats.append(cand[:S])
+        else:
+            seats.append([[cs for cs in cand if topo.mates(cs[0], lead[0]) or topo.chip(cs[0]) == topo.chip(lead[0])][0]
+                          for lead in seats[0]])
+
+    collect, finish = [], []
+    for gi, grp in enumerate(groups):
+        collect.append([])
+        finish.append([])
+        for cs in seats[gi]:
+            mate = [m for m in world if topo.mates(cs[0], m)][0]
+            port = [c for c in cs if c not in ranks and topo.die(c) == topo.die(grp[0]) and topo.may_write(c, mate)]
+            collect[gi].append(port[0])
+            finish[gi].append(port[1])
+
+    role = {}
+    for gi, grp in enumerate(groups):
+        for i, c in enumerate(grp):
+            role[c] = ("rank", gi, i)
+        for s in range(S):
+            role[collect[gi][s]] = ("collect", gi, s)
+            role[finish[gi][s]] = ("finish", gi, s)
+    plan = {"groups": groups, "collect": collect, "finish": finish, "role": role}
+    _CACHE["plan"] = plan
+    return plan
+
+
+def _split(topo, src, dsts):
+    far = [d for d in dsts if not _same_chip(topo, src, d)]
+    out = _join(_bits(topo.mask(src, far[0]))) if far else 0
+    masks = {}
+    for part, pool in ((far, _bits(out)), ([d for d in dsts if d not in far], None)):
+        if not part:
+            continue
+        if pool is None:
+            pool = _bits(topo.mask(src, part[0]) & ~out)
+        n = 1
+        while n * 2 * len(part) <= len(pool):
+            n *= 2
+        for i, d in enumerate(part):
+            masks[d] = _join(pool[i * n:(i + 1) * n])
+    return [masks[d] for d in dsts]
+
+
+def _near_far(topo, src, dsts):
+    far = [d for d in dsts if not _same_chip(topo, src, d)]
+    near = [d for d in dsts if d not in far]
+    m_far = 0
+    if far:
+        m_far = topo.mask(src, far[0])
+        for d in far:
+            m_far &= topo.mask(src, d)
+    m_near = (topo.mask(src, near[0]) & ~m_far) if near else 0
+    return [(far, m_far), (near, m_near)]
+
+
+def _fold_out(g, topo, core, srcs, dsts, slot, remote_sem, local_sem):
+    transfers, left = [], 0
+    for part, mask in _near_far(topo, core, dsts):
+        if not part:
+            continue
+        ids = []
+        for d in part:
+            rid, pid = topo.addr(d, core)
+            ids.append(DstId(rid=rid, pnc=pid))
+        transfers.append(RemoteDMATransfer(dst_ids=ids, dma_engine_mask=mask, remote_sem=remote_sem,
+                                           srcs=srcs, dsts=[slot for d in part], alu_op=ADD))
+        left += _count(mask)
+    g.remote_dma_fused(transfers, local_sem=local_sem)
+    return left
+
+
+def _mask_to(topo, src, dsts, d):
+    for part, mask in _near_far(topo, src, dsts):
+        if d in part:
+            return _count(mask)
+    return 0
+
+
+def _readers(plan, gi, s):
+    grp = plan["groups"][gi]
+    return [grp[(s + 1 + t) % len(grp)] for t in range(len(grp))]
+
+
+def rank_program(g, core, T, topo):
+    plan = _plan(T, topo)
+    if core not in plan["role"]:
+        return
+    kind, gi, k = plan["role"][core]
+    groups, collect, finish = plan["groups"], plan["collect"], plan["finish"]
+    sem = T.sem
+
+    if kind == "rank":
+        g.sync.dma_start(T.a_sb[:], T.a[:]).then_inc(sem.lda, 16)
+        g.scalar.dma_start(T.w_sb[:], T.w[:]).then_inc(sem.ldw, 16)
+        g.tensor.wait_ge(sem.lda, 16)
+        g.tensor.wait_ge(sem.ldw, 16)
+        for s in range(S):
+            g.tensor.matmul(T["ps%d" % s][:, 0:W], T.a_sb[:], T.w_sb[:, s * W:(s + 1) * W], True, True).then_inc(sem["mm%d" % s], 1)
+        for s in range(S):
+            g.vector.wait_ge(sem["mm%d" % s], 1)
+            g.vector.tensor_copy(T.p_sb[:, s * W:(s + 1) * W], T["ps%d" % s][:, 0:W]).then_inc(sem.cast, 1)
+        g.wait_ge(sem.cast, S)
+        masks = _split(topo, core, collect[gi])
+        transfers = []
+        for s in range(S):
+            rid, pid = topo.addr(collect[gi][s], core)
+            transfers.append(RemoteDMATransfer(dst_ids=[DstId(rid=rid, pnc=pid)], dma_engine_mask=masks[s], remote_sem=sem.raw,
+                                               src=T.p_sb[:, s * W:(s + 1) * W], dst=T.box[k]))
+        g.remote_dma_fused(transfers, local_sem=sem.sent)
+        order = sorted(range(S), key=lambda s: (not _same_chip(topo, finish[gi][s], core), _readers(plan, gi, s).index(core)))
+        for i, s in enumerate(order):
+            q = (g.sync, g.scalar)[i % 2]
+            q.wait_ge(sem["fin%d" % s], _mask_to(topo, finish[gi][s], groups[gi], core))
+            q.dma_start(T.y[:, s * W:(s + 1) * W], T.box[s]).then_inc(sem.stored, 16)
+        g.wait_ge(sem.sent, sum(_count(m) for m in masks))
+        g.wait_ge(sem.stored, 16 * S)
+
+    elif kind == "collect":
+        g.wait_ge(sem.raw, sum(_count(_split(topo, r, collect[gi])[k]) for r in groups[gi]))
+        left = _fold_out(g, topo, core, [T.box[i] for i in range(len(groups[gi]))], [f[k] for f in finish],
+                         T.box[gi], sem.sums, sem.sent)
+        g.wait_ge(sem.sent, left)
+
+    else:
+        g.wait_ge(sem.sums, sum(_mask_to(topo, collect[h][k], [f[k] for f in finish], core) for h in range(len(groups))))
+        left = _fold_out(g, topo, core, [T.box[h] for h in range(len(groups))], _readers(plan, gi, k),
+                         T.box[k], sem["fin%d" % k], sem.sent)
+        g.wait_ge(sem.sent, left)

@@ -3,6 +3,7 @@ from concourse.bass import DstId, RemoteDMATransfer
 S = 4
 W = 512 // S
 ADD = 1
+WAVES = [[0, 1], [2, 3]]
 
 SCRATCH = {
     "a_sb": ("sbuf", [128, 128], "bfloat16"),
@@ -14,7 +15,7 @@ SCRATCH = {
     "ps3": ("psum", [128, 512], "float32"),
     "box": ("dram", [5, 128, W], "bfloat16"),
 }
-SEMAPHORES = ["lda", "ldw", "mm0", "mm1", "mm2", "mm3", "cast", "sent", "raw", "sums",
+SEMAPHORES = ["lda", "ldw", "mm0", "mm1", "mm2", "mm3", "cast0", "cast1", "sent", "raw", "sums",
               "fin0", "fin1", "fin2", "fin3", "stored"]
 
 _CACHE = {}
@@ -171,27 +172,32 @@ def rank_program(g, core, T, topo):
         g.tensor.wait_ge(sem.ldw, 16)
         for s in range(S):
             g.tensor.matmul(T["ps%d" % s][:, 0:W], T.a_sb[:], T.w_sb[:, s * W:(s + 1) * W], True, True).then_inc(sem["mm%d" % s], 1)
-        for s in range(S):
-            g.vector.wait_ge(sem["mm%d" % s], 1)
-            g.vector.tensor_copy(T.p_sb[:, s * W:(s + 1) * W], T["ps%d" % s][:, 0:W]).then_inc(sem.cast, 1)
-        g.wait_ge(sem.cast, S)
-        masks = _split(topo, core, collect[gi])
-        transfers = []
-        for s in range(S):
-            rid, pid = topo.addr(collect[gi][s], core)
-            transfers.append(RemoteDMATransfer(dst_ids=[DstId(rid=rid, pnc=pid)], dma_engine_mask=masks[s], remote_sem=sem.raw,
-                                               src=T.p_sb[:, s * W:(s + 1) * W], dst=T.box[k]))
-        g.remote_dma_fused(transfers, local_sem=sem.sent)
-        order = sorted(range(S), key=lambda s: (not _same_chip(topo, finish[gi][s], core), _readers(plan, gi, s).index(core)))
-        for i, s in enumerate(order):
-            q = (g.sync, g.scalar)[i % 2]
-            q.wait_ge(sem["fin%d" % s], _mask_to(topo, finish[gi][s], groups[gi], core))
-            q.dma_start(T.y[:, s * W:(s + 1) * W], T.box[s]).then_inc(sem.stored, 16)
-        g.wait_ge(sem.sent, sum(_count(m) for m in masks))
+        for wave, part in enumerate(WAVES):
+            for s in part:
+                g.vector.wait_ge(sem["mm%d" % s], 1)
+                g.vector.tensor_copy(T.p_sb[:, s * W:(s + 1) * W], T["ps%d" % s][:, 0:W]).then_inc(sem["cast%d" % wave], 1)
+        left = 0
+        for wave, part in enumerate(WAVES):
+            g.wait_ge(sem["cast%d" % wave], len(part))
+            masks = _split(topo, core, [collect[gi][s] for s in part])
+            transfers = []
+            for s, mask in zip(part, masks):
+                rid, pid = topo.addr(collect[gi][s], core)
+                transfers.append(RemoteDMATransfer(dst_ids=[DstId(rid=rid, pnc=pid)], dma_engine_mask=mask, remote_sem=sem.raw,
+                                                   src=T.p_sb[:, s * W:(s + 1) * W], dst=T.box[k]))
+                left += _count(mask)
+            g.remote_dma_fused(transfers, local_sem=sem.sent)
+        for part in WAVES:
+            for i, s in enumerate(part):
+                q = (g.sync, g.scalar)[i % 2]
+                q.wait_ge(sem["fin%d" % s], _mask_to(topo, finish[gi][s], groups[gi], core))
+                q.dma_start(T.y[:, s * W:(s + 1) * W], T.box[s]).then_inc(sem.stored, 16)
+        g.wait_ge(sem.sent, left)
         g.wait_ge(sem.stored, 16 * S)
 
     elif kind == "collect":
-        g.wait_ge(sem.raw, sum(_count(_split(topo, r, collect[gi])[k]) for r in groups[gi]))
+        part = [p for p in WAVES if k in p][0]
+        g.wait_ge(sem.raw, sum(_count(_split(topo, r, [collect[gi][s] for s in part])[part.index(k)]) for r in groups[gi]))
         left = _fold_out(g, topo, core, [T.box[i] for i in range(len(groups[gi]))], [f[k] for f in finish],
                          T.box[gi], sem.sums, sem.sent)
         g.wait_ge(sem.sent, left)

@@ -82,11 +82,13 @@ def _plan(T, topo):
     for gi, grp in enumerate(groups):
         collect.append([])
         finish.append([])
-        for cs in seats[gi]:
+        for cs, lead in zip(seats[gi], seats[0]):
             mate = [m for m in world if topo.mates(cs[0], m)][0]
-            port = [c for c in cs if c not in ranks and topo.die(c) == topo.die(grp[0]) and topo.may_write(c, mate)]
-            collect[gi].append(port[0])
-            finish[gi].append(port[1])
+            port = [c for c in cs if c not in ranks and topo.may_write(c, mate)]
+            here = [c for c in port if topo.die(c) == topo.die(grp[0])]
+            there = [c for c in port if c not in here]
+            collect[gi].append(there[0] if topo.mates(cs[0], lead[0]) else here[0])
+            finish[gi].append(here[1])
 
     role = {}
     for gi, grp in enumerate(groups):
@@ -120,6 +122,7 @@ def _split(topo, src, dsts):
 def _near_far(topo, src, dsts):
     far = [d for d in dsts if not _same_chip(topo, src, d)]
     near = [d for d in dsts if d not in far]
+    far.sort(key=lambda d: topo.rack(topo.host(d)) == topo.rack(topo.host(src)))
     m_far = 0
     if far:
         m_far = topo.mask(src, far[0])

from concourse.bass import DstId, RemoteDMATransfer

S = 4
W = 512 // S
ADD = 1
WAVES = [[0, 1], [2, 3]]

SCRATCH = {
    "a_sb": ("sbuf", [128, 128], "bfloat16"),
    "w_sb": ("sbuf", [128, 512], "bfloat16"),
    "p_sb": ("sbuf", [128, 512], "bfloat16"),
    "ps0": ("psum", [128, 512], "float32"),
    "ps1": ("psum", [128, 512], "float32"),
    "ps2": ("psum", [128, 512], "float32"),
    "ps3": ("psum", [128, 512], "float32"),
    "box": ("dram", [5, 128, W], "bfloat16"),
}
SEMAPHORES = ["lda", "ldw", "mm0", "mm1", "mm2", "mm3", "cast0", "cast1", "sent", "raw", "sums",
              "fin0", "fin1", "fin2", "fin3", "stored"]

_CACHE = {}


def _bits(mask):
    return [1 << i for i in range(mask.bit_length()) if (mask >> i) & 1]


def _count(mask):
    return len(_bits(mask))


def _join(bits):
    m = 0
    for b in bits:
        m |= b
    return m


def _same_chip(topo, a, b):
    return topo.host(a) == topo.host(b) and topo.chip(a) == topo.chip(b)


def _plan(T, topo):
    if "plan" in _CACHE:
        return _CACHE["plan"]
    ranks = list(T.cores)
    hosts = list(range(max(topo.host(c) for c in ranks) + 1))
    world = range(len(hosts) * topo.CORES_PER_HOST)
    chips = {}
    for c in world:
        chips.setdefault((topo.host(c), topo.chip(c)), []).append(c)

    groups = []
    for c in ranks:
        home = [grp for grp in groups if topo.same_plane(c, grp[0])]
        if home:
            home[0].append(c)
        else:
            groups.append([c])
    groups.sort(key=lambda grp: -len(grp))

    first = {h: chips[(h, 0)][0] for h in hosts}
    combos = [[]]
    for grp in groups:
        near = [h for h in hosts if topo.rack(h) == topo.rack(topo.host(grp[0]))]
        combos = [c + [h] for c in combos for h in near]
    combos = [c for c in combos if all(topo.may_write(first[x], first[y]) for x in c for y in c)]
    hub = max(combos, key=lambda c: sum(topo.host(r) == h for grp, h in zip(groups, c) for r in grp))

    seats = []
    for gi, grp in enumerate(groups):
        cand = [cs for (h, k), cs in sorted(chips.items()) if h == hub[gi]
                and all(_same_chip(topo, r, cs[0]) or topo.same_plane(r, cs[0]) for r in grp)]
        if gi == 0:
            cand.sort(key=lambda cs: not any(r in cs for r in grp))
            seats.append(cand[:S])
        else:
            seats.append([[cs for cs in cand if topo.mates(cs[0], lead[0]) or topo.chip(cs[0]) == topo.chip(lead[0])][0]
                          for lead in seats[0]])

    collect, finish = [], []
    for gi, grp in enumerate(groups):
        collect.append([])
        finish.append([])
        for cs, lead in zip(seats[gi], seats[0]):
            mate = [m for m in world if topo.mates(cs[0], m)][0]
            port = [c for c in cs if c not in ranks and topo.may_write(c, mate)]
            here = [c for c in port if topo.die(c) == topo.die(grp[0])]
            there = [c for c in port if c not in here]
            collect[gi].append(there[0] if topo.mates(cs[0], lead[0]) else here[0])
            finish[gi].append(here[1])

    role = {}
    for gi, grp in enumerate(groups):
        for i, c in enumerate(grp):
            role[c] = ("rank", gi, i)
        for s in range(S):
            role[collect[gi][s]] = ("collect", gi, s)
            role[finish[gi][s]] = ("finish", gi, s)
    plan = {"groups": groups, "collect": collect, "finish": finish, "role": role}
    _CACHE["plan"] = plan
    return plan


def _split(topo, src, dsts):
    far = [d for d in dsts if not _same_chip(topo, src, d)]
    out = _join(_bits(topo.mask(src, far[0]))) if far else 0
    masks = {}
    for part, pool in ((far, _bits(out)), ([d for d in dsts if d not in far], None)):
        if not part:
            continue
        if pool is None:
            pool = _bits(topo.mask(src, part[0]) & ~out)
        n = 1
        while n * 2 * len(part) <= len(pool):
            n *= 2
        for i, d in enumerate(part):
            masks[d] = _join(pool[i * n:(i + 1) * n])
    return [masks[d] for d in dsts]


def _near_far(topo, src, dsts):
    far = [d for d in dsts if not _same_chip(topo, src, d)]
    near = [d for d in dsts if d not in far]
    far.sort(key=lambda d: topo.rack(topo.host(d)) == topo.rack(topo.host(src)))
    m_far = 0
    if far:
        m_far = topo.mask(src, far[0])
        for d in far:
            m_far &= topo.mask(src, d)
    m_near = (topo.mask(src, near[0]) & ~m_far) if near else 0
    return [(far, m_far), (near, m_near)]


def _fold_out(g, topo, core, srcs, dsts, slot, remote_sem, local_sem):
    transfers, left = [], 0
    for part, mask in _near_far(topo, core, dsts):
        if not part:
            continue
        ids = []
        for d in part:
            rid, pid = topo.addr(d, core)
            ids.append(DstId(rid=rid, pnc=pid))
        transfers.append(RemoteDMATransfer(dst_ids=ids, dma_engine_mask=mask, remote_sem=remote_sem,
                                           srcs=srcs, dsts=[slot for d in part], alu_op=ADD))
        left += _count(mask)
    g.remote_dma_fused(transfers, local_sem=local_sem)
    return left


def _mask_to(topo, src, dsts, d):
    for part, mask in _near_far(topo, src, dsts):
        if d in part:
            return _count(mask)
    return 0


def _readers(plan, gi, s):
    grp = plan["groups"][gi]
    return [grp[(s + 1 + t) % len(grp)] for t in range(len(grp))]


def rank_program(g, core, T, topo):
    plan = _plan(T, topo)
    if core not in plan["role"]:
        return
    kind, gi, k = plan["role"][core]
    groups, collect, finish = plan["groups"], plan["collect"], plan["finish"]
    sem = T.sem

    if kind == "rank":
        g.sync.dma_start(T.a_sb[:], T.a[:]).then_inc(sem.lda, 16)
        g.scalar.dma_start(T.w_sb[:], T.w[:]).then_inc(sem.ldw, 16)
        g.tensor.wait_ge(sem.lda, 16)
        g.tensor.wait_ge(sem.ldw, 16)
        for s in range(S):
            g.tensor.matmul(T["ps%d" % s][:, 0:W], T.a_sb[:], T.w_sb[:, s * W:(s + 1) * W], True, True).then_inc(sem["mm%d" % s], 1)
        for wave, part in enumerate(WAVES):
            for s in part:
                g.vector.wait_ge(sem["mm%d" % s], 1)
                g.vector.tensor_copy(T.p_sb[:, s * W:(s + 1) * W], T["ps%d" % s][:, 0:W]).then_inc(sem["cast%d" % wave], 1)
        left = 0
        for wave, part in enumerate(WAVES):
            g.wait_ge(sem["cast%d" % wave], len(part))
            masks = _split(topo, core, [collect[gi][s] for s in part])
            transfers = []
            for s, mask in zip(part, masks):
                rid, pid = topo.addr(collect[gi][s], core)
                transfers.append(RemoteDMATransfer(dst_ids=[DstId(rid=rid, pnc=pid)], dma_engine_mask=mask, remote_sem=sem.raw,
                                                   src=T.p_sb[:, s * W:(s + 1) * W], dst=T.box[k]))
                left += _count(mask)
            g.remote_dma_fused(transfers, local_sem=sem.sent)
        for part in WAVES:
            for i, s in enumerate(part):
                q = (g.sync, g.scalar)[i % 2]
                q.wait_ge(sem["fin%d" % s], _mask_to(topo, finish[gi][s], groups[gi], core))
                q.dma_start(T.y[:, s * W:(s + 1) * W], T.box[s]).then_inc(sem.stored, 16)
        g.wait_ge(sem.sent, left)
        g.wait_ge(sem.stored, 16 * S)

    elif kind == "collect":
        part = [p for p in WAVES if k in p][0]
        g.wait_ge(sem.raw, sum(_count(_split(topo, r, [collect[gi][s] for s in part])[part.index(k)]) for r in groups[gi]))
        left = _fold_out(g, topo, core, [T.box[i] for i in range(len(groups[gi]))], [f[k] for f in finish],
                         T.box[gi], sem.sums, sem.sent)
        g.wait_ge(sem.sent, left)

    else:
        g.wait_ge(sem.sums, sum(_mask_to(topo, collect[h][k], [f[k] for f in finish], core) for h in range(len(groups))))
        left = _fold_out(g, topo, core, [T.box[h] for h in range(len(groups))], _readers(plan, gi, k),
                         T.box[k], sem["fin%d" % k], sem.sent)
        g.wait_ge(sem.sent, left)
